import numpy as np, ml_dtypes
CORES = [16,17,18,19,32,33,34,35]
N = 8
BF = ml_dtypes.bfloat16
def gentries(a):
    return np.ascontiguousarray(a.reshape(8, 16, -1).transpose(0, 2, 1)).reshape(8, -1)
def gtable(e):
    e = np.asarray(e); return np.ascontiguousarray(e.reshape(8, -1, 16).transpose(0, 2, 1)).reshape(128, -1).astype(np.int32)
def f(rng, *shape):
    return (rng.standard_normal(shape, dtype=np.float32) * np.exp2(rng.integers(-2, 3, shape[:-1] + (1,)))).astype(BF)
def wide(rng, *shape):
    v = f(rng, *shape).astype(np.float32); k = shape[:-2] + (1, shape[-1])
    return (v * np.exp2(rng.integers(-6, 7, k)) * (rng.random(k) > 0.0625)).astype(BF)
LV, M, S = 4, 768, 32
R, A = LV * M, (LV - 1) * (N - 1) * S
W, K = R + A, 4 * M * (LV - 1)
LEV4 = np.repeat(np.concatenate([np.arange(R) // M, np.arange(A) // ((N - 1) * S)]), 4)
OWN4 = np.repeat(np.arange(W) < R, 4).astype(np.float64)
def draw_ent(rng, pri, tidy):
    e = np.zeros((8, LV - 1, 4, M), np.int64)
    for g in range(8):
        free = np.ones(4 * W, bool)
        for l in range(1, LV):
            c = np.flatnonzero(free & (LEV4 < l)); c = c[np.argsort(pri[c] + rng.random(len(c)))[:4 * M]]; free[c] = False
            e[g, l - 1] = np.sort(c).reshape(M, 4)[rng.permutation(M)].T if tidy else rng.permutation(c).reshape(4, M)
    return gtable(e.reshape(8, -1))
def draw_sl(rng, same):
    s = np.zeros((8, LV - 1, N - 1, S), np.int64)
    for g in range(8):
        for l in range(LV - 1):
            if same:
                u = np.concatenate([[0, M - 1], 1 + rng.permutation(M - 2)[:S - 2]]); v = [rng.permutation(u) for d in range(N - 1)]
            else:
                v = [rng.permutation(M)[:S] for d in range(N - 1)]
            s[g, l] = l * M + np.stack(v)
    return gtable(s.reshape(8, -1))
def draw(rng, pri, tidy, same):
    return {"b": f(rng, N, 128, R), "val": ((rng.random((N, 8, K)) - 0.5) * 0.5).astype(BF),
            "ent": np.stack([draw_ent(rng, pri[r], tidy[r]) for r in range(N)]), "sl": np.stack([draw_sl(rng, same) for r in range(N)])}
def setup_inputs(rng):
    return draw(rng, [0 * OWN4] * N, [False] * N, False)
def setup_inputs_same(rng):
    return draw(rng, [OWN4] * N, [False] * N, True)
def setup_inputs_old(rng):
    return draw(rng, [LEV4.astype(np.float64)] * N, [False] * N, False)
def setup_inputs_mixed(rng):
    o = int(rng.integers(0, 2))
    return draw(rng, [1 - OWN4 if (r + o) % 2 else OWN4 for r in range(N)], [(r + o) % 2 == 1 for r in range(N)], False)
def setup_inputs_strong(rng):
    d = setup_inputs(rng); d["val"] = np.where(rng.random((N, 8, K)) < 0.9, -0.25, 0.25).astype(BF); return d
def setup_inputs_spread(rng):
    d = setup_inputs(rng); d["b"] = wide(rng, N, 128, R)
    d["val"] = (d["val"].astype(np.float32) * np.exp2(-rng.integers(0, 7, (N, 8, K))) * (rng.random((N, 8, K)) > 0.0625)).astype(BF); return d
def check_inputs(d):
    bad = []
    if not np.isfinite(d["b"].astype(np.float32)).all(): bad.append("b finite")
    if not (np.abs(d["val"].astype(np.float32)) <= 0.25).all(): bad.append("size of val")
    lv = np.arange(LV - 1)
    for r in range(N):
        e = gentries(d["ent"][r]).astype(np.int64); s = gentries(d["sl"][r]).astype(np.int64).reshape(8, LV - 1, N - 1, S)
        if (e < 0).any() or (e >= 4 * W).any(): bad.append("ent range")
        elif (LEV4[e].reshape(8, LV - 1, 4 * M) > lv[:, None]).any(): bad.append("ent level")
        if (np.diff(np.sort(e, axis=1), axis=1) == 0).any(): bad.append("ent differ")
        if (s // M != lv[:, None, None]).any(): bad.append("sl level")
        if (np.diff(np.sort(s, axis=3), axis=3) == 0).any(): bad.append("sl differ")
    return sorted(set(bad))
def reference(b, val, ent, sl):
    en = np.stack([gentries(ent[r]) for r in range(N)]).astype(np.int64).reshape(N, 8, LV - 1, 4, M); place = en // 4
    se = np.stack([gentries(sl[r]) for r in range(N)]).astype(np.int64).reshape(N, 8, LV - 1, N - 1, S)
    v = val.astype(np.float64).reshape(N, 8, LV - 1, 4, M)
    w = np.zeros((N, 8, 16, W), np.float64); w[..., :R] = b.astype(np.float64).reshape(N, 8, 16, R)
    for l in range(LV):
        for r in range(N):
            for g in range(8):
                if l > 0: w[r, g, :, l * M:(l + 1) * M] -= np.sum(v[r, g, l - 1] * w[r, g][:, place[r, g, l - 1]], axis=1)
                if l < LV - 1:
                    for d in range(N - 1):
                        m = R + (l * (N - 1) + d) * S
                        w[(r + 1 + d) % N, g, :, m:m + S] = w[r, g][:, se[r, g, l, d]]
    z = np.zeros((N, 8, 16, R), np.float64); bk = np.zeros((N, 8, 16, 4 * W), np.float64)
    for l in range(LV - 1, -1, -1):
        for r in range(N):
            for g in range(8):
                x = w[r, g, :, l * M:(l + 1) * M] - np.sum(bk[r, g, :, 4 * l * M:4 * (l + 1) * M].reshape(16, M, 4), axis=2)
                if l < LV - 1:
                    for d in range(N - 1):
                        m = R + (l * (N - 1) + d) * S
                        x[:, se[r, g, l, d] - l * M] -= np.sum(bk[(r + 1 + d) % N, g, :, 4 * m:4 * (m + S)].reshape(16, S, 4), axis=2)
                z[r, g, :, l * M:(l + 1) * M] = x
                if l > 0: bk[r, g][:, en[r, g, l - 1]] = v[r, g, l - 1] * x[:, None, :]
    return {"z": z.reshape(N, 128, R).astype(np.float32)}

from concourse.bass import DstId, RemoteDMATransfer
from concourse.mybir import AluOpType, ActivationFunctionType

N, M, S, LV = 8, 768, 32, 4
R = M * LV
F = (N - 1) * S
MK, FK = M // 16, F // 16
P0 = 64
LAND0 = 1024

SCRATCH = {
    "pv": ("psum", [128, 4 * M], "float32"),
    "pa": ("psum", [128, 1024], "float32"),
    "yw": ("sbuf", [128, R + 3 * F], "float32"),
    "w0": ("sbuf", [128, LAND0 + F], "bfloat16"),
    "bb": ("sbuf", [128, 3 * M], "bfloat16"),
    "pp": ("sbuf", [128, P0 + 12 * M], "float32"),
    "tt": ("sbuf", [128, 4 * M], "float32"),
    "vs": ("sbuf", [128, 12 * M], "bfloat16"),
    "vc": ("sbuf", [128, 12 * M], "bfloat16"),
    "ei": ("sbuf", [128, 12 * MK], "int32"),
    "si": ("sbuf", [128, 3 * FK], "int32"),
    "so": ("sbuf", [128, 3 * FK], "uint16"),
    "pf": ("sbuf", [128, 12 * MK], "uint16"),
    "pos": ("sbuf", [128, 12 * MK], "uint16"),
    "ia": ("sbuf", [128, 8 * MK], "int32"),
    "ib": ("sbuf", [128, 4 * MK], "int32"),
    "ic": ("sbuf", [128, 4 * MK], "int32"),
    "ie": ("sbuf", [128, 4 * MK], "int32"),
    "ig": ("sbuf", [128, 4 * MK], "int32"),
    "seli": ("sbuf", [128, 128], "int32"),
    "sel": ("sbuf", [128, 128], "bfloat16"),
    "idi": ("sbuf", [128, 128], "int32"),
    "negi": ("sbuf", [128, 128], "float32"),
    "idb": ("sbuf", [128, 128], "bfloat16"),
    "sb0": ("sbuf", [128, F], "bfloat16"),
    "sbf": ("sbuf", [128, 5 * F], "float32"),
    "rb": ("sbuf", [128, 3 * F], "float32"),
    "rt": ("sbuf", [128, F], "float32"),
    "mo": ("sbuf", [128, 4, MK], "float32"),
    "mf": ("sbuf", [128, 4, FK], "float32"),
}
for _l in (1, 2, 3):
    SCRATCH["tb%d" % _l] = ("sbuf", [128, 64 * (MK + FK) * _l], "float32")
    SCRATCH["dd%d" % _l] = ("sbuf", [128, 4, (MK + FK) * _l], "float32")
    SCRATCH["ol%d" % (_l - 1)] = ("sbuf", [128, 4 * MK], "uint16")
    SCRATCH["fl%d" % (_l - 1)] = ("sbuf", [128, 4 * FK], "uint16")

POOL = {"v": 14, "s": 8, "p": 8, "g": 14}
NDMA = 20
SEMAPHORES = (["%s%d" % (q, k) for q in POOL for k in range(POOL[q])] + ["d%d" % k for k in range(NDMA)]
              + ["fa%d" % h for h in range(3)] + ["ba%d_%d" % (h, d) for h in range(3) for d in range(N - 1)] + ["sent"])

ADD, SUB, MUL = AluOpType.add, AluOpType.subtract, AluOpType.mult
ACT = ActivationFunctionType


def engine_plan(src, dsts, topo):
    far = [c for c in dsts if topo.chip(c) != topo.chip(src)]
    near = [c for c in dsts if topo.chip(c) == topo.chip(src)]
    fe = topo.engines(src, far[0])
    per = len(fe) // len(far)
    ne = [e for e in topo.engines(src, near[0]) if e not in fe]
    plan = {}
    for k, c in enumerate(far):
        plan[c] = fe[k * per:(k + 1) * per]
    for k, c in enumerate(near):
        plan[c] = ne[k * per:(k + 1) * per]
    return plan


def rank_program(g, core, T, topo):
    rank = T.rank_of(core)
    if rank is None:
        return
    cores = list(T.cores)
    Q = {"v": g.vector, "s": g.scalar, "p": g.tensor, "g": g, "y": g.sync}
    total, seen, turn, nd = {}, {q: {} for q in Q}, {q: 0 for q in POOL}, [0]

    def wait(q, *toks):
        for name, n in toks:
            if seen[q].get(name, 0) < n:
                Q[q].wait_ge(T.sem[name], n)
                seen[q][name] = n

    def done(q, *makers):
        name = "%s%d" % (q, turn[q] % POOL[q])
        turn[q] += 1
        wait(q, (name, total.get(name, 0)))
        for mk in makers:
            mk().then_inc(T.sem[name], 1)
            total[name] = total.get(name, 0) + 1
        return (name, total[name])

    def dma(q, *pairs):
        name = "d%d" % nd[0]
        nd[0] += 1
        for out, src in pairs:
            Q[q].dma_start(out, src).then_inc(T.sem[name], 16)
            total[name] = total.get(name, 0) + 16
        return (name, total[name])

    V, A, PE = g.vector, g.scalar, g.tensor
    others = lambda c: [x for x in cores if x != c]
    plan = engine_plan(core, others(core), topo)
    engines_in = lambda src: len(engine_plan(src, others(src), topo)[core])

    def send(pieces):
        ts = []
        for dst_core, src, dst, sem in pieces:
            rid, pid, _ = topo.addr(dst_core)
            ts.append(RemoteDMATransfer(dst_ids=[DstId(rid=rid, pnc=pid)], dma_engine_mask=sum(1 << e for e in plan[dst_core]),
                                        remote_sem=T.sem[sem], src=src, dst=dst))
            total["sent"] = total.get("sent", 0) + len(plan[dst_core])
        g.remote_dma_fused(ts, local_sem=T.sem.sent)

    fa = []
    for h in range(3):
        total["fa%d" % h] = sum(engines_in(c) for c in others(core))
        fa.append(("fa%d" % h, total["fa%d" % h]))
    ba = {}
    for h in range(3):
        for d in range(N - 1):
            name = "ba%d_%d" % (h, d)
            total[name] = engines_in(cores[(rank + 1 + d) % N])
            ba[h, d] = (name, total[name])
    d_order = sorted(range(N - 1), key=lambda d: topo.chip(cores[(rank + 1 + d) % N]) != topo.chip(core))

    ylev = lambda h: T.yw[:, M * h:M * (h + 1)]
    j0 = lambda l, e: 4 * M * (l - 1) + M * e
    psl = lambda l, e: T.pp[:, P0 + j0(l, e):P0 + j0(l, e) + M]
    lcol = lambda l, e: slice(j0(l, e) // 16, j0(l, e) // 16 + MK)
    tsl = lambda e: T.tt[:, M * e:M * (e + 1)]
    tb = {l: T["tb%d" % l] for l in (1, 2, 3)}
    dd = {l: T["dd%d" % l] for l in (1, 2, 3)}
    zw = {l: 4 * (MK + FK) * l for l in (1, 2, 3)}
    zc = {3: 2 * M, 2: 2 * M + zw[3], 1: 2 * M + zw[3] + zw[2]}

    l_sl = dma("y", (T.si[:], T.sl[:]))
    l_b0 = dma("y", (T.w0[:, 0:LAND0], T.b[:, 0:LAND0]))
    l_ent = dma("s", (T.ei[:], T.ent[:]))
    l_vc = dma("s", (T.vc[0:8, :], T.val[:]))
    z_a = done("v", lambda: V.memset(T.yw[:, zc[3]:zc[2]], 0.0))
    z_b = done("v", lambda: V.memset(T.yw[:, zc[2]:R], 0.0), lambda: V.memset(T.pp[:, 0:P0], 0.0))

    def clear(l, tok):
        wait("y", tok)
        return dma("y", (tb[l][0:128:16, :], T.yw[:, zc[l]:zc[l] + zw[l]]))

    init = {3: clear(3, z_a)}
    g_sel = done("g", lambda: g.iota(T.seli[0:8, :], [[1, 8], [0, 16]], 0, -1))
    g_id = done("g", lambda: g.iota(T.idi[:], [[-1, 128]], 0, 1))
    pay = {}

    def payload(l, e):
        pay[l, e] = done("g", lambda: g.iota(psl(l, e), [[1, M]], P0 + j0(l, e), 0, allow_small_or_imprecise_dtypes=True))

    payload(3, 0)
    wait("v", g_sel)
    c_sel = done("v", lambda: V.tensor_scalar(T.sel[0:8, :], T.seli[0:8, :], 0.0, -1.0, AluOpType.is_equal, MUL))

    def spread(l):
        base = j0(l, 0)
        mm = lambda k: (lambda: PE.matmul(T.pv[:, 512 * k:512 * (k + 1)], T.sel[0:8, :], T.vc[0:8, base + 512 * k:base + 512 * (k + 1)], True, True))
        return done("p", mm(0), mm(1), mm(2)), done("p", mm(3), mm(4), mm(5))

    wait("p", c_sel, l_vc)
    pv_a, pv_b = spread(1)
    wait("s", pv_a)
    vs_a = done("s", lambda: A.activation(T.vs[:, 0:2 * M], T.pv[:, 0:2 * M], ACT.Identity, scale=-1.0))
    wait("s", pv_b)
    vs_b = done("s", lambda: A.activation(T.vs[:, 2 * M:4 * M], T.pv[:, 2 * M:4 * M], ACT.Identity, scale=-1.0))
    wait("p", vs_a, vs_b)
    pv_tok = spread(3)

    wait("v", l_sl)
    so = {0: done("v", lambda: V.tensor_copy(T.so[:, 0:FK], T.si[:, 0:FK]))}
    wait("v", so[0], l_b0)
    sh = done("v", lambda: V.tensor_copy(T.sb0[:], T.w0[:, 0:M].indirect(T.so[:, 0:FK])))
    wait("g", sh)
    send([(cores[(rank + 1 + d) % N], T.sb0[:, S * d:S * (d + 1)], T.w0[:, LAND0 + S * d:LAND0 + S * (d + 1)], "fa0") for d in range(N - 1)])
    for l, e in ((3, 1), (3, 2), (3, 3), (2, 0)):
        payload(l, e)

    scratch_free = []

    def positions(l):
        K = (MK + FK) * l
        e_ = T.ei[:, 4 * MK * (l - 1):4 * MK * l]
        hi, lo, th, u = T.ib[:], T.ic[:], T.ie[:], T.ig[:]
        wait("v", *scratch_free)
        t1 = done("v", lambda: V.tensor_scalar(lo, e_, 63, None, AluOpType.bitwise_and))
        t2 = done("v", lambda: V.tensor_scalar(hi, e_, 6, None, AluOpType.arith_shift_right),
                  lambda: V.tensor_scalar(th, e_, float(4 * R), float(-(LV - l) * MK), AluOpType.is_ge, MUL))
        wait("v", t1)
        t3 = done("v", lambda: V.tensor_scalar(u, lo, float(K), None, MUL))
        wait("v", t2)
        t4 = done("v", lambda: V.tensor_tensor(hi, hi, th, ADD))
        wait("v", t3, t4)
        t5 = done("v", lambda: V.tensor_tensor(u, u, hi, ADD))
        wait("v", t5)
        t6 = done("v", lambda: V.tensor_copy(T.pos[:, 4 * MK * (l - 1):4 * MK * l], u))
        scratch_free.append(t6)
        return t6

    wait("v", l_ent)
    pos = {3: positions(3)}
    t = done("v", lambda: V.tensor_scalar(T.ia[:, 0:4 * MK], T.ei[:, 0:4 * MK], 2, 2047, AluOpType.arith_shift_right, AluOpType.bitwise_and))
    wait("v", g_id)
    c_id = done("v", lambda: V.tensor_scalar(T.negi[:], T.idi[:], 0.0, -1.0, AluOpType.is_equal, MUL),
                lambda: V.tensor_scalar(T.idb[:], T.idi[:], 0.0, None, AluOpType.is_equal))
    wait("v", t)
    pf1 = done("v", lambda: V.tensor_copy(T.pf[:, 0:4 * MK], T.ia[:, 0:4 * MK]))
    y0 = done("v", lambda: V.tensor_copy(ylev(0), T.w0[:, 0:M]),
              lambda: V.tensor_scalar(T.so[:, FK:2 * FK], T.si[:, FK:2 * FK], float(-M), None, ADD),
              lambda: V.tensor_scalar(T.so[:, 2 * FK:3 * FK], T.si[:, 2 * FK:3 * FK], float(-2 * M), None, ADD))
    wait("v", pf1)
    t = done("v", lambda: V.tensor_scalar(T.ia[:], T.ei[:, 4 * MK:12 * MK], 2, None, AluOpType.arith_shift_right))
    wait("v", t)
    pf23 = done("v", lambda: V.tensor_copy(T.pf[:, 4 * MK:12 * MK], T.ia[:]))

    inv = {}

    def invert(l, es, after=()):
        wait("s", pos[l], init[l], *after)
        for e in es:
            wait("s", pay[l, e], *([inv[l]] if l in inv else []))
            inv[l] = done("s", lambda: A.activation(tb[l][:].indirect(T.pos[:, lcol(l, e)]), psl(l, e), ACT.Silu))

    invert(3, range(4))

    def load_b(l):
        return dma("y", (T.bb[:, M * (l - 1):M * l], T.b[:, M * l:M * (l + 1)]))

    def load_val(l):
        cols = slice(j0(l, 0), j0(l, 0) + 4 * M)
        return dma("y", *[(T.vs[c:128:16, cols], T.val[:, cols]) for c in range(16)])

    def dump(q, l):
        wait(q, inv[l])
        return dma(q, (dd[l][:], tb[l][0:128:16, :]))

    def lists(h, toks):
        wait("v", *toks)
        own = lambda l: dd[l][:, :, MK * h:MK * (h + 1)]
        frn = lambda l: dd[l][:, :, MK * l + FK * h:MK * l + FK * (h + 1)]
        a, b_ = own(3), frn(3)
        for l in range(2, h, -1):
            t = done("v", lambda: V.tensor_tensor(T.mo[:], a, own(l), ADD), lambda: V.tensor_tensor(T.mf[:], b_, frn(l), ADD))
            wait("v", t)
            a, b_ = T.mo[:], T.mf[:]
        return done("v", lambda: V.tensor_scalar(T["fl%d" % h][:], b_, 0.25, None, ADD),
                    lambda: V.tensor_scalar(T["ol%d" % h][:], a, 0.25, None, ADD))

    banks = ((0, 512), (512, M))
    pa_free = []
    vs_tok = {1: [vs_a, vs_b]}
    dmp, lst = {}, {}

    for l in (1, 2, 3):
        wait("y", fa[l - 1])
        lb = load_b(l)
        if l < 3:
            init[3 - l] = clear(3 - l, z_b)
            vs_tok[l + 1] = [load_val(l + 1)]
        else:
            dmp[3] = dump("y", 3)
        win = T.w0[:] if l == 1 else T.yw[:, 0:R + F * l]
        wait("v", pf1, pf23, y0, z_a, z_b, *vs_tok[l])
        wait("v", fa[l - 1])
        tk = []
        for e in range(4):
            tk.append(done("v", lambda: V.tensor_tensor(tsl(e), win.indirect(T.pf[:, lcol(l, e)]), T.vs[:, j0(l, e):j0(l, e) + M], MUL)))
        wait("p", c_id, *pa_free)
        mm = []
        for e in range(2):
            wait("p", tk[e])
            mm.append(done("p", *[(lambda a=a, b_=b_: PE.matmul(T.pa[:, a:b_], T.negi[:], T.tt[:, M * e + a:M * e + b_], e == 0, False)) for a, b_ in banks]))
        wait("p", lb)
        mm.append(done("p", *[(lambda a=a, b_=b_: PE.matmul(T.pa[:, a:b_], T.idb[:], T.bb[:, M * (l - 1) + a:M * (l - 1) + b_], False, True)) for a, b_ in banks]))
        if l == 3:
            lst[2] = lists(2, [dmp[3]])
        wait("v", tk[2], *mm)
        u = done("v", lambda: V.tensor_tensor(T.pa[:, 0:M], T.pa[:, 0:M], tsl(2), SUB))
        wait("v", tk[0], tk[1], tk[3], u, *([init[3], init[2]] if l == 2 else [init[1]] if l == 3 else []))
        yl = done("v", lambda: V.tensor_tensor(ylev(l), T.pa[:, 0:M], tsl(3), SUB))
        pa_free = [yl]
        wait("v", yl)
        if l == 3:
            break
        out = T.sbf[:, F * (l - 1):F * l]
        sh = done("v", lambda: V.tensor_copy(out, ylev(l).indirect(T.so[:, FK * l:FK * (l + 1)])))
        wait("g", sh)
        send([(cores[(rank + 1 + d) % N], T.sbf[:, F * (l - 1) + S * d:F * (l - 1) + S * (d + 1)],
               T.yw[:, R + F * l + S * d:R + F * l + S * (d + 1)], "fa%d" % l) for d in range(N - 1)])
        if l == 1:
            for l2, e in ((2, 1), (2, 2), (2, 3), (1, 0)):
                payload(l2, e)
            f0 = done("v", lambda: V.tensor_copy(T.yw[:, R:R + F], T.w0[:, LAND0:LAND0 + F]))
            pos[2] = positions(2)
            pos[1] = positions(1)
            wait("v", f0)
            invert(2, range(4))
        else:
            for e in (1, 2, 3):
                payload(1, e)
            wait("v", pos[1], init[1], pay[1, 0])
            v_inv = done("v", lambda: V.tensor_copy(tb[1][:].indirect(T.pos[:, lcol(1, 0)]), psl(1, 0)))

    dmp[2] = dump("y", 2)
    zl = yl
    wait("v", *pay.values())
    wait("s", z_b, *pay.values())

    for l in (3, 2, 1):
        h = l - 1
        wait("y", zl)
        dma("y", (T.z[:, M * l:M * (l + 1)], ylev(l)))
        wait("v", zl, lst[h], *pv_tok)
        pm = done("v", *[(lambda e=e: V.tensor_tensor(psl(l, e), ylev(l), T.pv[:, M * e:M * (e + 1)], MUL)) for e in range(4)])
        wait("v", pm)
        win = T.pp[:]
        fl, ol = T["fl%d" % h], T["ol%d" % h]
        c0 = F * (2 + h)
        out = T.sbf[:, c0:c0 + F]
        t = done("v", lambda: V.tensor_copy(out, win.indirect(fl[:, 0:FK])))
        for s in (1, 2, 3):
            wait("v", t)
            t = done("v", lambda: V.tensor_tensor(out, win.indirect(fl[:, FK * s:FK * (s + 1)]), out, ADD))
        wait("g", t)
        send([(cores[(rank - 1 - d) % N], T.sbf[:, c0 + S * d:c0 + S * (d + 1)],
               T.rb[:, F * h + S * d:F * h + S * (d + 1)], "ba%d_%d" % (h, d)) for d in range(N - 1)])
        wait("s", pm, lst[h], *pa_free)
        sg = [done("s", lambda: A.activation(tsl(s), win.indirect(ol[:, MK * s:MK * (s + 1)]), ACT.Identity)) for s in (2, 3)]
        wait("p", pm)
        if l > 1:
            pv_tok = spread(l - 1)
        wait("p", *pa_free)
        mm = []
        for k, s in enumerate((2, 3)):
            wait("p", sg[k])
            mm.append(done("p", *[(lambda a=a, b_=b_: PE.matmul(T.pa[:, a:b_], T.negi[:], T.tt[:, M * s + a:M * s + b_], k == 0, k == 1)) for a, b_ in banks]))
        if l == 3:
            invert(1, (1, 2, 3), [v_inv])
            dmp[1] = dump("s", 1)
        t = done("v", lambda: V.tensor_tensor(ylev(h), win.indirect(ol[:, 0:MK]), ylev(h), ADD))
        wait("v", t)
        t = done("v", lambda: V.tensor_tensor(ylev(h), win.indirect(ol[:, MK:2 * MK]), ylev(h), ADD))
        wait("v", t, *mm)
        t = done("v", lambda: V.tensor_tensor(ylev(h), ylev(h), T.pa[:, 0:M], SUB))
        pa_free = [t]
        if h > 0:
            lst[h - 1] = lists(h - 1, [dmp[h]])
        for d in d_order:
            off = T.so[:, FK * h + 2 * d:FK * h + 2 * d + 2]
            wait("v", t, ba[h, d])
            t = done("v", lambda: V.tensor_tensor(T.rt[:, S * d:S * (d + 1)], ylev(h).indirect(off), T.rb[:, F * h + S * d:F * h + S * (d + 1)], ADD))
            wait("v", t)
            t = done("v", lambda: V.tensor_copy(ylev(h).indirect(off), T.rt[:, S * d:S * (d + 1)]))
        zl = t

    wait("y", zl)
    dma("y", (T.z[:, 0:M], ylev(0)))
    for name in total:
        if max(seen[q].get(name, 0) for q in seen) < total[name]:
            wait("g", (name, total[name]))
